import numpy as np
import ml_dtypes


def mxq(x, axis, fmt="e4m3"):
    dtype, down = {"e4m3": (ml_dtypes.float8_e4m3fn, 7), "e5m2": (ml_dtypes.float8_e5m2, 14)}[fmt]
    v = np.moveaxis(np.asarray(x, np.float32).astype(ml_dtypes.bfloat16).astype(np.float64), axis, -1)
    blocks = v.reshape(v.shape[:-1] + (-1, 32))
    amax = np.abs(blocks).max(-1, keepdims=True)
    byte = np.maximum(np.where(amax > 0, np.frexp(amax)[1] - 1 + 127, 0) - down, 1)
    scale = np.exp2(byte - 127.0)
    codes = (blocks / scale).astype(np.float32).astype(dtype).astype(np.float64)
    return np.moveaxis((codes * scale).reshape(v.shape), -1, axis)


WIDE = False


def mx_kscale(k):
    if not WIDE:
        return np.ones(k)
    levels = np.array([10, -10, 5, -5, 0])
    if k % 512:
        return np.exp2(np.random.permutation(np.resize(levels, k // 32))).repeat(32)
    a = np.empty((k // 512, 16))
    for p in range(k // 512):
        a[p, :8] = np.random.permutation(np.resize(levels, 8))
        for g in range(8):
            far = levels[np.abs(levels - a[p, g]) >= 10]
            a[p, g + 8] = far[np.random.randint(len(far))]
    return np.exp2(a.ravel()).repeat(32)


def f64(x):
    return np.asarray(x).astype(np.float64)


def striped(idx):
    return np.tile(idx.reshape(-1, 16).T, (8, 1)).astype(np.uint16)


def unstriped(offs):
    return offs[:16].T.reshape(-1).astype(np.int64)


def striped8(idx):
    return np.concatenate([x.reshape(-1, 16).T for x in idx]).astype(np.uint16)


def runs(offs, k):
    lists = np.stack([offs[16 * r : 16 * r + 16].T.reshape(-1) for r in range(8)]).astype(np.int64)
    return lists[np.arange(k) % 512 // 64]


def pack_weight(w):
    k, n = w.shape
    w = f64(np.asarray(w, np.float32).astype(ml_dtypes.bfloat16)).reshape(k // 32, 32, n)
    amax = np.abs(w).max(1)
    byte = np.clip(np.where(amax > 0, np.frexp(amax)[1] - 1 + 127 - 7, 1), 1, 254)
    scaled = (w * np.exp2(127.0 - byte)[:, None, :]).reshape(k, n).astype(np.float32)
    words = np.ascontiguousarray(scaled.reshape(k // 512, 128, 4, n).transpose(0, 1, 3, 2)).astype(ml_dtypes.float8_e4m3fn).view(np.uint8)
    return words, np.ascontiguousarray(byte.astype(np.uint8).reshape(k // 512, 16, n))


def unpack_weight(words, scales):
    g, p, n, _ = words.shape
    vals = np.ascontiguousarray(words).view(ml_dtypes.float8_e4m3fn).astype(np.float64) * np.repeat(np.exp2(scales.astype(np.float64) - 127.0), 8, axis=1)[..., None]
    return vals.transpose(0, 1, 3, 2).reshape(g * 512, n)


K, T, S, N, H, G, W = 512, 2048, 512, 512, 512, 2048, 256


def setup_inputs():
    n = np.random.standard_normal
    s = mx_kscale(K)[:, None]
    u = mx_kscale(S)
    packed_xT = pack_weight(n((K, T)) * s)
    packed_dT = pack_weight(n((K, G)) / s)
    perm = np.stack([np.random.permutation(S) for _ in range(8)])
    return {
        "x_words": packed_xT[0],
        "x_scales": packed_xT[1],
        "w1": (n((K, H)) / np.sqrt(K) / s).astype(np.float32),
        "d_words": packed_dT[0],
        "d_scales": packed_dT[1],
        "gn": (np.random.uniform(0.5, 1.5, (H, 1)) * u[:, None]).astype(np.float32),
        "w2": (n((H, N)) / np.sqrt(H) / u[:, None]).astype(np.float32),
        "offs": striped(np.random.permutation(T)[:S]),
        "k1": striped8(np.random.randint(0, G, (8, H))),
        "two": striped(np.random.permutation(T)[:S]),
        "n1": striped(np.random.permutation(S)),
        "n2": striped(np.random.permutation(S)),
        "n3": striped8(perm[:, :W]),
        "n4": striped8(perm[:, W:]),
    }


def reference(x_words, x_scales, w1, d_words, d_scales, gn, w2, offs, k1, two, n1, n2, n3, n4):
    xq = unpack_weight(x_words, x_scales)[:, unstriped(offs)]
    y = mxq(f64(w1), 0, "e4m3").T @ xq
    d_k1 = unpack_weight(d_words, d_scales)[np.arange(K)[:, None], runs(k1, K)]
    x_two = unpack_weight(x_words, x_scales)[:, unstriped(two)]
    d = 0.0625 * (d_k1.T @ x_two)
    z = f64(gn) * (y[:, unstriped(n1)] - (np.tanh(d) * d[:, unstriped(n2)]))
    h = mxq(f64(w2), 0, "e4m3").T @ mxq(z, 0, "e4m3")
    pb = h[np.arange(N)[:, None], runs(n4, N)]
    pa = h[np.arange(N)[:, None], runs(n3, N)]
    rb = pb - (0.5 * pa)
    ra = np.sqrt((pa) ** 2 + (pb) ** 2 + 0.25)
    ds = np.zeros((N, S))
    ds[np.arange(N)[:, None], runs(n3, N)] = ra
    out = ds.copy()
    out[np.arange(N)[:, None], runs(n4, N)] = rb
    return out

@@ -1,0 +1,226 @@
+from contextlib import ExitStack
+
+import concourse.mybir as mybir
+
+F32 = mybir.dt.float32
+BF16 = mybir.dt.bfloat16
+I32 = mybir.dt.int32
+U32 = mybir.dt.uint32
+U16 = mybir.dt.uint16
+U8 = mybir.dt.uint8
+FP8X4 = mybir.dt.float8_e4m3fn_x4
+ACT = mybir.ActivationFunctionType
+ALU = mybir.AluOpType
+
+P = 128
+PACK = 4
+TABLE = 2048
+S = 512
+HALF = S // 2
+SHIFT = 14
+SHIFTED = 112
+FIRST = 512
+FLOPS = 3 * 2 * 512 * 512 * 512
+
+
+def tile_picked_twkeysoftbpolar_none_p_kernel(
+    tc, x_words, x_scales, w1, d_words, d_scales, gn, w2, offs, k1, two, n1, n2, n3, n4, out
+):
+    nc = tc.nc
+    with ExitStack() as ctx:
+        lists = ctx.enter_context(tc.tile_pool(name="lists", bufs=1))
+        keep = ctx.enter_context(tc.tile_pool(name="keep", bufs=1))
+        psum = ctx.enter_context(tc.psum_pool(name="psum", bufs=1))
+
+        def load_list(source, name):
+            held = lists.tile(list(source.shape), U16, name=name)
+            nc.sync.dma_start(held[:], source)
+            return held
+
+        def sbuf(shape, dtype, name, tag=""):
+            return keep.tile(shape, dtype, name=name, tag=tag, align_bytes=64)
+
+        d_byte_table = sbuf([P, TABLE], U8, "d_byte_table")
+        x_byte_table = sbuf([P, TABLE], U8, "x_byte_table")
+        d_word_table = sbuf([P, TABLE], U32, "d_word_table")
+        x_word_table = sbuf([P, TABLE], U32, "x_word_table")
+        d_scale_plane = sbuf([P, S], U8, "d_scale_plane")
+        nc.vector.memset(d_byte_table[:].bitcast(I32), 0)
+        nc.vector.memset(x_byte_table[:].bitcast(I32), 0)
+        nc.vector.memset(d_scale_plane[:].bitcast(I32), 0)
+
+        d_words_hbm = d_words[0].rearrange("p n t -> p (n t)").bitcast(I32)
+        k1_list = load_list(k1, "k1_list")
+        nc.sync.dma_start(d_word_table[:].bitcast(I32)[:, :FIRST], d_words_hbm[:, :FIRST])
+        for q in range(4):
+            nc.sync.dma_start(
+                d_byte_table[:].bitcast(I32)[32 * q + SHIFT : 32 * q + SHIFT + 4, :],
+                d_scales[0].bitcast(I32)[4 * q : 4 * q + 4, :],
+            )
+        nc.sync.dma_start(d_word_table[:].bitcast(I32)[:, FIRST:], d_words_hbm[:, FIRST:])
+        two_list = load_list(two, "two_list")
+        for q in range(4):
+            nc.sync.dma_start(
+                x_byte_table[:].bitcast(I32)[32 * q : 32 * q + 4, :],
+                x_scales[0].bitcast(I32)[4 * q : 4 * q + 4, :],
+            )
+        nc.sync.dma_start(x_word_table[:].bitcast(I32), x_words[0].rearrange("p n t -> p (n t)").bitcast(I32))
+        offs_list = load_list(offs, "offs_list")
+        gain = sbuf([P, PACK], F32, "gain")
+        nc.sync.dma_start(gain[:], gn.rearrange("(p t) o -> p (t o)", t=PACK))
+        n2_list = load_list(n2, "n2_list")
+        n1_list = load_list(n1, "n1_list")
+        n3_list = load_list(n3, "n3_list")
+        n4_list = load_list(n4, "n4_list")
+        w1_raw = sbuf([P, PACK, S], F32, "w1_raw", tag="w_raw")
+        nc.sync.dma_start(w1_raw[:], w1.rearrange("(p j) c -> p j c", j=PACK))
+
+        d_gain = sbuf([P, PACK], F32, "d_gain")
+        nc.gpsimd.tensor_scalar(d_gain[:], gain[:], -0.0625, 0.0, ALU.mult, ALU.add)
+
+        def pick(table, offsets, dtype, name):
+            picked = sbuf([P, S], dtype, name)
+            nc.vector.tensor_copy(picked[:], table[:].indirect(offsets[:]))
+            return picked
+
+        def deal(picked, dtype, name):
+            dealt = sbuf([P, S], dtype, name)
+            nc.vector.tensor_copy(
+                dealt[:].rearrange("p (t m) -> p m t", t=PACK), picked[:].rearrange("p (m t) -> p m t", t=PACK)
+            )
+            return dealt
+
+        d_bytes = deal(pick(d_byte_table, k1_list, U8, "d_bytes_picked"), U8, "d_bytes")
+        nc.scalar.dma_start(
+            d_scale_plane[:].bitcast(I32)[0:SHIFTED, :], d_bytes[:].bitcast(I32)[SHIFT : SHIFT + SHIFTED, :]
+        )
+        d_codes = deal(pick(d_word_table, k1_list, U32, "d_words_picked"), U32, "d_codes")
+        two_bytes = pick(x_byte_table, two_list, U8, "two_bytes")
+        two_codes = pick(x_word_table, two_list, U32, "two_codes")
+
+        def product(bank, width, lhs_codes, lhs_bytes, rhs_codes, rhs_bytes):
+            acc = psum.tile([P, width], F32, name="acc", tag="bank%d" % bank)
+            nc.tensor.matmul_mx(
+                out=acc[:],
+                lhsT=lhs_codes.bitcast(FP8X4),
+                lhsT_scale=lhs_bytes,
+                rhs=rhs_codes.bitcast(FP8X4),
+                rhs_scale=rhs_bytes,
+                start=True,
+                stop=True,
+            )
+            return acc
+
+        cols = [slice(P * t, P * (t + 1)) for t in range(PACK)]
+        d_acc = [
+            product(t, S, d_codes[:, cols[t]], d_scale_plane[:, cols[t]], two_codes[:], two_bytes[:])
+            for t in range(PACK)
+        ]
+
+        x_bytes = pick(x_byte_table, offs_list, U8, "x_bytes")
+        x_codes = pick(x_word_table, offs_list, U32, "x_codes")
+        w1_bf = sbuf([P, PACK * S], BF16, "w1_bf")
+        nc.vector.tensor_copy(
+            w1_bf[:].rearrange("p (t m j) -> p m j t", t=PACK, j=PACK),
+            w1_raw[:].rearrange("p j (m t) -> p m j t", t=PACK),
+        )
+        w2_raw = sbuf([P, PACK, S], F32, "w2_raw", tag="w_raw")
+        nc.sync.dma_start(w2_raw[:], w2.rearrange("(p j) c -> p j c", j=PACK))
+
+        def quantize(values, width, name):
+            codes = sbuf([P, width], U32, name + "_codes")
+            scale_bytes = sbuf([P, width], U8, name + "_bytes")
+            nc.vector.quantize_mx(out=codes[:].bitcast(FP8X4), scales=scale_bytes[:], in_=values)
+            return codes, scale_bytes
+
+        y_acc = []
+        for t in range(PACK):
+            w1_codes, w1_bytes = quantize(w1_bf[:, S * t : S * (t + 1)], P, "w1_%d" % t)
+            y_acc.append(product(PACK + t, S, w1_codes[:], w1_bytes[:], x_codes[:], x_bytes[:]))
+
+        tanh_d = sbuf([P, PACK, S], F32, "tanh_d")
+        d_rows = [sbuf([P, S], F32, "d_rows%d" % t) for t in range(PACK)]
+        y_rows = [sbuf([P, S], F32, "y_rows%d" % t, tag="y_rows%d" % t) for t in range(PACK)]
+        for t in range(PACK):
+            nc.scalar.activation(d_rows[t][:], d_acc[t][:], ACT.Copy, scale=d_gain[:, t : t + 1])
+            nc.scalar.activation(tanh_d[:, t, :], d_acc[t][:], ACT.Tanh, scale=0.0625)
+        for t in range(PACK):
+            nc.vector.tensor_scalar_mul(y_rows[t][:], y_acc[t][:], gain[:, t : t + 1])
+
+        w2_by_tile = w2_raw[:].rearrange("p j (u t r) -> p t u j r", t=PACK, r=4)
+
+        def w2_tile(t):
+            w2_bf = sbuf([P, PACK * P], BF16, "w2_bf%d" % t, tag="y_rows%d" % t)
+            nc.scalar.copy(w2_bf[:].rearrange("p (u r j) -> p u j r", r=4, j=PACK), w2_by_tile[:, t])
+            return quantize(w2_bf[:], P, "w2_%d" % t)
+
+        d_got = sbuf([P, PACK, HALF], F32, "d_got")
+        y_got = [sbuf([P, PACK, HALF], F32, "y_got%d" % half) for half in range(2)]
+        pull = [sbuf([P, PACK, HALF], F32, "pull%d" % half) for half in range(2)]
+        entries = [slice(half * HALF // 16, (half + 1) * HALF // 16) for half in range(2)]
+        places = [slice(half * HALF, (half + 1) * HALF) for half in range(2)]
+        for t in range(PACK):
+            nc.scalar.activation(d_got[:, t, :], d_rows[t][:].indirect(n2_list[:, entries[0]]), ACT.Copy)
+        for half in range(2):
+            for t in range(PACK):
+                nc.scalar.activation(y_got[half][:, t, :], y_rows[t][:].indirect(n1_list[:, entries[half]]), ACT.Copy)
+        for t in range(PACK):
+            nc.vector.tensor_tensor(
+                pull[1][:, t, :], d_rows[t][:].indirect(n2_list[:, entries[1]]), tanh_d[:, t, places[1]], ALU.mult
+            )
+        nc.vector.tensor_tensor(pull[0][:], d_got[:], tanh_d[:, :, places[0]], ALU.mult)
+
+        w2_mx = [w2_tile(0)]
+        z_mx = []
+        for half in range(2):
+            z_bf = sbuf([P, PACK * HALF], BF16, "z_bf%d" % half, tag="z_bf")
+            nc.vector.tensor_tensor(
+                z_bf[:].rearrange("p (c i t) -> p c t i", i=4, t=PACK),
+                y_got[half][:].rearrange("p t (c i) -> p c t i", i=4),
+                pull[half][:].rearrange("p t (c i) -> p c t i", i=4),
+                ALU.add,
+            )
+            z_mx.append(quantize(z_bf[:], HALF, "z_%d" % half))
+        for t in range(1, PACK):
+            w2_mx.append(w2_tile(t))
+
+        out_by_tile = out.rearrange("(u t r) c -> t u r c", t=PACK, r=4)
+        h_rows = [sbuf([P, S], F32, "h_rows%d" % t) for t in range(PACK)]
+        result = [sbuf([P, S], F32, "result%d" % t) for t in range(PACK)]
+        radius_sq = [sbuf([P, HALF], F32, "radius_sq%d" % t) for t in range(PACK)]
+
+        def h_half(t, half):
+            return product(2 * t + half, HALF, w2_mx[t][0][:], w2_mx[t][1][:], z_mx[half][0][:], z_mx[half][1][:])
+
+        for t in range(PACK):
+            nc.scalar.copy(h_rows[t][:, places[0]], h_half(t, 0)[:])
+
+        def pair_up(t):
+            acc = h_half(t, 1)
+            pb = sbuf([P, HALF], F32, "pb%d" % t)
+            minus_half_pa = sbuf([P, HALF], F32, "minus_half_pa%d" % t)
+            if t == 0:
+                nc.vector.tensor_copy(h_rows[t][:, places[1]], acc[:])
+                nc.vector.tensor_copy(pb[:], h_rows[t][:].indirect(n4_list[:]))
+            else:
+                nc.scalar.copy(h_rows[t][:, places[1]], acc[:])
+                nc.scalar.activation(pb[:], h_rows[t][:].indirect(n4_list[:]), ACT.Copy)
+            nc.scalar.activation(minus_half_pa[:], h_rows[t][:].indirect(n3_list[:]), ACT.Copy, scale=-0.5)
+            nc.vector.tensor_tensor(result[t][:].indirect(n4_list[:]), pb[:], minus_half_pa[:], ALU.add)
+            pa_sq = sbuf([P, HALF], F32, "pa_sq%d" % t)
+            pb_sq = sbuf([P, HALF], F32, "pb_sq%d" % t)
+            nc.scalar.activation(pa_sq[:], minus_half_pa[:], ACT.Square, scale=-2.0)
+            nc.scalar.activation(pb_sq[:], pb[:], ACT.Square)
+            nc.vector.scalar_tensor_tensor(radius_sq[t][:], pa_sq[:], 0.25, pb_sq[:], ALU.add, ALU.add)
+
+        def finish(t):
+            ra = sbuf([P, HALF], F32, "ra%d" % t)
+            nc.scalar.activation(ra[:], radius_sq[t][:], ACT.Sqrt)
+            nc.vector.tensor_copy(result[t][:].indirect(n3_list[:]), ra[:])
+            nc.sync.dma_start(out_by_tile[t], result[t][:])
+
+        for t in range(PACK):
+            pair_up(t)
+            if t > 0:
+                finish(t - 1)
+        finish(PACK - 1)

@@ -20,6 +20,8 @@ HALF = S // 2
 SHIFT = 14
 SHIFTED = 112
 FIRST = 512
+PIECES = ((0, 256), (256, 128), (384, 128))
+Y_ON_SCALAR = 3
 FLOPS = 3 * 2 * 512 * 512 * 512
 
 
@@ -49,6 +51,9 @@ def tile_picked_twkeysoftbpolar_none_p_kernel(
         nc.vector.memset(x_byte_table[:].bitcast(I32), 0)
         nc.vector.memset(d_scale_plane[:].bitcast(I32), 0)
 
+        quarter = sbuf([P, 1], F32, "quarter")
+        nc.gpsimd.memset(quarter[:], 0.25)
+
         d_words_hbm = d_words[0].rearrange("p n t -> p (n t)").bitcast(I32)
         k1_list = load_list(k1, "k1_list")
         nc.sync.dma_start(d_word_table[:].bitcast(I32)[:, :FIRST], d_words_hbm[:, :FIRST])
@@ -66,8 +71,11 @@ def tile_picked_twkeysoftbpolar_none_p_kernel(
             )
         nc.sync.dma_start(x_word_table[:].bitcast(I32), x_words[0].rearrange("p n t -> p (n t)").bitcast(I32))
         offs_list = load_list(offs, "offs_list")
-        gain = sbuf([P, PACK], F32, "gain")
-        nc.sync.dma_start(gain[:], gn.rearrange("(p t) o -> p (t o)", t=PACK))
+        gain = sbuf([P, PACK, 8], F32, "gain")
+        gn_by_tile = gn.rearrange("(u t r) o -> t u r o", t=PACK, r=4)
+        for t in range(PACK):
+            with nc.allow_non_contiguous_dma(reason="128 gains, one value a partition"):
+                nc.gpsimd.dma_start(gain[:, t, 0:1], gn_by_tile[t])
         n2_list = load_list(n2, "n2_list")
         n1_list = load_list(n1, "n1_list")
         n3_list = load_list(n3, "n3_list")
@@ -76,27 +84,28 @@ def tile_picked_twkeysoftbpolar_none_p_kernel(
         nc.sync.dma_start(w1_raw[:], w1.rearrange("(p j) c -> p j c", j=PACK))
 
         d_gain = sbuf([P, PACK], F32, "d_gain")
-        nc.gpsimd.tensor_scalar(d_gain[:], gain[:], -0.0625, 0.0, ALU.mult, ALU.add)
+        nc.gpsimd.tensor_scalar(d_gain[:], gain[:, :, 0], -0.0625, 0.0, ALU.mult, ALU.add)
 
         def pick(table, offsets, dtype, name):
-            picked = sbuf([P, S], dtype, name)
-            nc.vector.tensor_copy(picked[:], table[:].indirect(offsets[:]))
+            picked = sbuf([P, 16 * offsets.shape[1]], dtype, name)
+            nc.vector.tensor_copy(picked[:], table[:].indirect(offsets))
             return picked
 
-        def deal(picked, dtype, name):
-            dealt = sbuf([P, S], dtype, name)
-            nc.vector.tensor_copy(
-                dealt[:].rearrange("p (t m) -> p m t", t=PACK), picked[:].rearrange("p (m t) -> p m t", t=PACK)
-            )
-            return dealt
-
-        d_bytes = deal(pick(d_byte_table, k1_list, U8, "d_bytes_picked"), U8, "d_bytes")
+        d_bytes_picked = pick(d_byte_table, k1_list[:], U8, "d_bytes_picked")
+        d_bytes = sbuf([P, S], U8, "d_bytes")
+        nc.vector.tensor_copy(
+            d_bytes[:].bitcast(I32).rearrange("p (t u) -> p t u", t=PACK),
+            d_bytes_picked[:].bitcast(I32).rearrange("p (u t) -> p t u", t=PACK),
+        )
         nc.scalar.dma_start(
             d_scale_plane[:].bitcast(I32)[0:SHIFTED, :], d_bytes[:].bitcast(I32)[SHIFT : SHIFT + SHIFTED, :]
         )
-        d_codes = deal(pick(d_word_table, k1_list, U32, "d_words_picked"), U32, "d_codes")
-        two_bytes = pick(x_byte_table, two_list, U8, "two_bytes")
-        two_codes = pick(x_word_table, two_list, U32, "two_codes")
+        d_words_picked = pick(d_word_table, k1_list[:], U32, "d_words_picked")
+        d_codes = sbuf([P, S], U32, "d_codes")
+        nc.vector.tensor_copy(
+            d_codes[:].rearrange("p (t u r) -> p t u r", t=PACK, r=4),
+            d_words_picked[:].rearrange("p (u t r) -> p t u r", t=PACK, r=4),
+        )
 
         def product(bank, width, lhs_codes, lhs_bytes, rhs_codes, rhs_bytes):
             acc = psum.tile([P, width], F32, name="acc", tag="bank%d" % bank)
@@ -112,20 +121,31 @@ def tile_picked_twkeysoftbpolar_none_p_kernel(
             return acc
 
         cols = [slice(P * t, P * (t + 1)) for t in range(PACK)]
-        d_acc = [
-            product(t, S, d_codes[:, cols[t]], d_scale_plane[:, cols[t]], two_codes[:], two_bytes[:])
-            for t in range(PACK)
-        ]
+        entries = [slice(half * HALF // 16, (half + 1) * HALF // 16) for half in range(2)]
+        places = [slice(half * HALF, (half + 1) * HALF) for half in range(2)]
+        tanh_d = sbuf([P, PACK, S], F32, "tanh_d")
+        d_rows = [sbuf([P, S], F32, "d_rows%d" % t) for t in range(PACK)]
+        for half in range(2):
+            two_bytes = pick(x_byte_table, two_list[:, entries[half]], U8, "two_bytes%d" % half)
+            two_codes = pick(x_word_table, two_list[:, entries[half]], U32, "two_codes%d" % half)
+            for t in range(PACK):
+                acc = product(
+                    PACK * (1 - half) + t, HALF, d_codes[:, cols[t]], d_scale_plane[:, cols[t]], two_codes[:], two_bytes[:]
+                )
+                nc.scalar.activation(tanh_d[:, t, places[half]], acc[:], ACT.Tanh, scale=0.0625)
+                nc.scalar.activation(d_rows[t][:, places[half]], acc[:], ACT.Copy, scale=d_gain[:, t : t + 1])
 
-        x_bytes = pick(x_byte_table, offs_list, U8, "x_bytes")
-        x_codes = pick(x_word_table, offs_list, U32, "x_codes")
-        w1_bf = sbuf([P, PACK * S], BF16, "w1_bf")
+        x_bytes = pick(x_byte_table, offs_list[:], U8, "x_bytes")
+        x_codes = pick(x_word_table, offs_list[:], U32, "x_codes")
+        w1_bf = sbuf([P, PACK * S], BF16, "w1_bf", tag="w1_bf")
         nc.vector.tensor_copy(
-            w1_bf[:].rearrange("p (t m j) -> p m j t", t=PACK, j=PACK),
-            w1_raw[:].rearrange("p j (m t) -> p m j t", t=PACK),
+            w1_bf[:].rearrange("p (t u r j) -> p t u j r", t=PACK, r=4, j=PACK),
+            w1_raw[:].rearrange("p j (u t r) -> p t u j r", t=PACK, r=4),
         )
         w2_raw = sbuf([P, PACK, S], F32, "w2_raw", tag="w_raw")
-        nc.sync.dma_start(w2_raw[:], w2.rearrange("(p j) c -> p j c", j=PACK))
+        w2_by_slot = w2.rearrange("(u j r) c -> j u r c", j=PACK, r=4)
+        for j in range(PACK):
+            nc.sync.dma_start(w2_raw[:, j, :], w2_by_slot[j])
 
         def quantize(values, width, name):
             codes = sbuf([P, width], U32, name + "_codes")
@@ -134,93 +154,106 @@ def tile_picked_twkeysoftbpolar_none_p_kernel(
             return codes, scale_bytes
 
         y_acc = []
-        for t in range(PACK):
-            w1_codes, w1_bytes = quantize(w1_bf[:, S * t : S * (t + 1)], P, "w1_%d" % t)
-            y_acc.append(product(PACK + t, S, w1_codes[:], w1_bytes[:], x_codes[:], x_bytes[:]))
+        for first in range(0, PACK, 2):
+            w1_codes, w1_bytes = quantize(w1_bf[:, S * first : S * (first + 2)], 2 * P, "w1_%d" % first)
+            for i in range(2):
+                y_acc.append(
+                    product(PACK + first + i, S, w1_codes[:, cols[i]], w1_bytes[:, cols[i]], x_codes[:], x_bytes[:])
+                )
 
-        tanh_d = sbuf([P, PACK, S], F32, "tanh_d")
-        d_rows = [sbuf([P, S], F32, "d_rows%d" % t) for t in range(PACK)]
         y_rows = [sbuf([P, S], F32, "y_rows%d" % t, tag="y_rows%d" % t) for t in range(PACK)]
         for t in range(PACK):
-            nc.scalar.activation(d_rows[t][:], d_acc[t][:], ACT.Copy, scale=d_gain[:, t : t + 1])
-            nc.scalar.activation(tanh_d[:, t, :], d_acc[t][:], ACT.Tanh, scale=0.0625)
-        for t in range(PACK):
-            nc.vector.tensor_scalar_mul(y_rows[t][:], y_acc[t][:], gain[:, t : t + 1])
+            if t < Y_ON_SCALAR:
+                nc.scalar.activation(y_rows[t][:], y_acc[t][:], ACT.Copy, scale=gain[:, t, 0:1])
+            else:
+                nc.vector.tensor_scalar_mul(y_rows[t][:], y_acc[t][:], gain[:, t, 0:1])
 
-        w2_by_tile = w2_raw[:].rearrange("p j (u t r) -> p t u j r", t=PACK, r=4)
-
-        def w2_tile(t):
-            w2_bf = sbuf([P, PACK * P], BF16, "w2_bf%d" % t, tag="y_rows%d" % t)
-            nc.scalar.copy(w2_bf[:].rearrange("p (u r j) -> p u j r", r=4, j=PACK), w2_by_tile[:, t])
-            return quantize(w2_bf[:], P, "w2_%d" % t)
-
-        d_got = sbuf([P, PACK, HALF], F32, "d_got")
-        y_got = [sbuf([P, PACK, HALF], F32, "y_got%d" % half) for half in range(2)]
-        pull = [sbuf([P, PACK, HALF], F32, "pull%d" % half) for half in range(2)]
-        entries = [slice(half * HALF // 16, (half + 1) * HALF // 16) for half in range(2)]
-        places = [slice(half * HALF, (half + 1) * HALF) for half in range(2)]
-        for t in range(PACK):
-            nc.scalar.activation(d_got[:, t, :], d_rows[t][:].indirect(n2_list[:, entries[0]]), ACT.Copy)
+        y_got = [sbuf([P, PACK, width], F32, "y_got%d" % start) for start, width in PIECES]
+        for got, (start, width) in zip(y_got, PIECES):
+            piece_entries = slice(start // 16, (start + width) // 16)
+            for t in range(PACK):
+                nc.scalar.activation(got[:, t, :], y_rows[t][:].indirect(n1_list[:, piece_entries]), ACT.Copy)
+        pull = sbuf([P, PACK, S], F32, "pull", tag="w1_bf")
         for half in range(2):
             for t in range(PACK):
-                nc.scalar.activation(y_got[half][:, t, :], y_rows[t][:].indirect(n1_list[:, entries[half]]), ACT.Copy)
-        for t in range(PACK):
-            nc.vector.tensor_tensor(
-                pull[1][:, t, :], d_rows[t][:].indirect(n2_list[:, entries[1]]), tanh_d[:, t, places[1]], ALU.mult
-            )
-        nc.vector.tensor_tensor(pull[0][:], d_got[:], tanh_d[:, :, places[0]], ALU.mult)
+                nc.vector.tensor_tensor(
+                    pull[:, t, places[half]],
+                    d_rows[t][:].indirect(n2_list[:, entries[half]]),
+                    tanh_d[:, t, places[half]],
+                    ALU.mult,
+                )
 
-        w2_mx = [w2_tile(0)]
+        w2_by_tile = w2_raw[:].rearrange("p j (u t r) -> p t u j r", t=PACK, r=4)
+        w2_mx = {}
+
+        def w2_tile(t):
+            w2_bf = sbuf([P, S], BF16, "w2_bf%d" % t, tag="y_rows%d" % t)
+            nc.scalar.copy(w2_bf[:].rearrange("p (u r j) -> p u j r", r=4, j=PACK), w2_by_tile[:, t])
+            w2_mx[t] = quantize(w2_bf[:], P, "w2_%d" % t)
+
         z_mx = []
-        for half in range(2):
-            z_bf = sbuf([P, PACK * HALF], BF16, "z_bf%d" % half, tag="z_bf")
+        for got, (start, width) in zip(y_got, PIECES):
+            z_bf = sbuf([P, PACK * width], BF16, "z_bf%d" % start)
             nc.vector.tensor_tensor(
                 z_bf[:].rearrange("p (c i t) -> p c t i", i=4, t=PACK),
-                y_got[half][:].rearrange("p t (c i) -> p c t i", i=4),
-                pull[half][:].rearrange("p t (c i) -> p c t i", i=4),
+                got[:].rearrange("p t (c i) -> p c t i", i=4),
+                pull[:, :, start : start + width].rearrange("p t (c i) -> p c t i", i=4),
                 ALU.add,
             )
-            z_mx.append(quantize(z_bf[:], HALF, "z_%d" % half))
-        for t in range(1, PACK):
-            w2_mx.append(w2_tile(t))
+            z_mx.append(quantize(z_bf[:], width, "z_%d" % start))
 
         out_by_tile = out.rearrange("(u t r) c -> t u r c", t=PACK, r=4)
-        h_rows = [sbuf([P, S], F32, "h_rows%d" % t) for t in range(PACK)]
-        result = [sbuf([P, S], F32, "result%d" % t) for t in range(PACK)]
-        radius_sq = [sbuf([P, HALF], F32, "radius_sq%d" % t) for t in range(PACK)]
 
         def h_half(t, half):
-            return product(2 * t + half, HALF, w2_mx[t][0][:], w2_mx[t][1][:], z_mx[half][0][:], z_mx[half][1][:])
+            acc = psum.tile([P, HALF], F32, name="acc", tag="bank%d" % (2 * t + half))
+            for (z_codes, z_bytes), (start, width) in zip(z_mx, PIECES):
+                if start // HALF == half:
+                    nc.tensor.matmul_mx(
+                        out=acc[:, start % HALF : start % HALF + width],
+                        lhsT=w2_mx[t][0][:].bitcast(FP8X4),
+                        lhsT_scale=w2_mx[t][1][:],
+                        rhs=z_codes[:].bitcast(FP8X4),
+                        rhs_scale=z_bytes[:],
+                        start=True,
+                        stop=True,
+                    )
+            return acc
 
-        for t in range(PACK):
-            nc.scalar.copy(h_rows[t][:, places[0]], h_half(t, 0)[:])
+        def pair_up(first):
+            pair = (first, first + 1)
+            h_rows = {t: sbuf([P, S], F32, "h_rows%d" % t) for t in pair}
+            result = {t: sbuf([P, S], F32, "result%d" % t) for t in pair}
+            pb = {t: sbuf([P, HALF], F32, "pb%d" % t) for t in pair}
+            minus_half_pa = {t: sbuf([P, HALF], F32, "minus_half_pa%d" % t) for t in pair}
+            for t in pair:
+                w2_tile(t)
+                nc.scalar.copy(h_rows[t][:, places[0]], h_half(t, 0)[:])
+            for t in pair:
+                if t == 0:
+                    nc.vector.tensor_copy(h_rows[t][:, places[1]], h_half(t, 1)[:])
+                    nc.vector.tensor_copy(pb[t][:], h_rows[t][:].indirect(n4_list[:]))
+                else:
+                    nc.scalar.copy(h_rows[t][:, places[1]], h_half(t, 1)[:])
+            for t in pair:
+                nc.scalar.activation(minus_half_pa[t][:], h_rows[t][:].indirect(n3_list[:]), ACT.Copy, scale=-0.5)
+                if t > 0:
+                    nc.scalar.activation(pb[t][:], h_rows[t][:].indirect(n4_list[:]), ACT.Copy)
+                rb = sbuf([P, HALF], F32, "rb%d" % t)
+                adder = nc.vector if t == 0 else nc.gpsimd
+                adder.tensor_tensor(rb[:], pb[t][:], minus_half_pa[t][:], ALU.add)
+                nc.vector.tensor_copy(result[t][:].indirect(n4_list[:]), rb[:])
+            radius_sq = {t: sbuf([P, HALF], F32, "radius_sq%d" % t) for t in pair}
+            for t in pair:
+                pa_sq = sbuf([P, HALF], F32, "pa_sq%d" % t)
+                pb_sq = sbuf([P, HALF], F32, "pb_sq%d" % t)
+                nc.scalar.activation(pa_sq[:], minus_half_pa[t][:], ACT.Square, scale=-2.0)
+                nc.scalar.activation(pb_sq[:], pb[t][:], ACT.Square)
+                nc.gpsimd.tensor_tensor(radius_sq[t][:], pa_sq[:], pb_sq[:], ALU.add)
+            for t in pair:
+                ra = sbuf([P, HALF], F32, "ra%d" % t)
+                nc.scalar.activation(ra[:], radius_sq[t][:], ACT.Sqrt, bias=quarter[:])
+                nc.vector.tensor_copy(result[t][:].indirect(n3_list[:]), ra[:])
+                nc.sync.dma_start(out_by_tile[t], result[t][:])
 
-        def pair_up(t):
-            acc = h_half(t, 1)
-            pb = sbuf([P, HALF], F32, "pb%d" % t)
-            minus_half_pa = sbuf([P, HALF], F32, "minus_half_pa%d" % t)
-            if t == 0:
-                nc.vector.tensor_copy(h_rows[t][:, places[1]], acc[:])
-                nc.vector.tensor_copy(pb[:], h_rows[t][:].indirect(n4_list[:]))
-            else:
-                nc.scalar.copy(h_rows[t][:, places[1]], acc[:])
-                nc.scalar.activation(pb[:], h_rows[t][:].indirect(n4_list[:]), ACT.Copy)
-            nc.scalar.activation(minus_half_pa[:], h_rows[t][:].indirect(n3_list[:]), ACT.Copy, scale=-0.5)
-            nc.vector.tensor_tensor(result[t][:].indirect(n4_list[:]), pb[:], minus_half_pa[:], ALU.add)
-            pa_sq = sbuf([P, HALF], F32, "pa_sq%d" % t)
-            pb_sq = sbuf([P, HALF], F32, "pb_sq%d" % t)
-            nc.scalar.activation(pa_sq[:], minus_half_pa[:], ACT.Square, scale=-2.0)
-            nc.scalar.activation(pb_sq[:], pb[:], ACT.Square)
-            nc.vector.scalar_tensor_tensor(radius_sq[t][:], pa_sq[:], 0.25, pb_sq[:], ALU.add, ALU.add)
-
-        def finish(t):
-            ra = sbuf([P, HALF], F32, "ra%d" % t)
-            nc.scalar.activation(ra[:], radius_sq[t][:], ACT.Sqrt)
-            nc.vector.tensor_copy(result[t][:].indirect(n3_list[:]), ra[:])
-            nc.sync.dma_start(out_by_tile[t], result[t][:])
-
-        for t in range(PACK):
-            pair_up(t)
-            if t > 0:
-                finish(t - 1)
-        finish(PACK - 1)
+        for first in range(0, PACK, 2):
+            pair_up(first)

@@ -17,9 +17,7 @@ PACK = 4
 TABLE = 2048
 S = 512
 HALF = S // 2
-SHIFT = 14
-SHIFTED = 112
-FIRST = 512
+FIRST = 256
 PIECES = ((0, 256), (256, 128), (384, 128))
 Y_ON_SCALAR = 3
 FLOPS = 3 * 2 * 512 * 512 * 512
@@ -49,21 +47,17 @@ def tile_picked_twkeysoftbpolar_none_p_kernel(
         d_scale_plane = sbuf([P, S], U8, "d_scale_plane")
         nc.vector.memset(d_byte_table[:].bitcast(I32), 0)
         nc.vector.memset(x_byte_table[:].bitcast(I32), 0)
-        nc.vector.memset(d_scale_plane[:].bitcast(I32), 0)
 
         quarter = sbuf([P, 1], F32, "quarter")
         nc.gpsimd.memset(quarter[:], 0.25)
 
         d_words_hbm = d_words[0].rearrange("p n t -> p (n t)").bitcast(I32)
         k1_list = load_list(k1, "k1_list")
-        nc.sync.dma_start(d_word_table[:].bitcast(I32)[:, :FIRST], d_words_hbm[:, :FIRST])
-        for q in range(4):
-            nc.sync.dma_start(
-                d_byte_table[:].bitcast(I32)[32 * q + SHIFT : 32 * q + SHIFT + 4, :],
-                d_scales[0].bitcast(I32)[4 * q : 4 * q + 4, :],
-            )
-        nc.sync.dma_start(d_word_table[:].bitcast(I32)[:, FIRST:], d_words_hbm[:, FIRST:])
         two_list = load_list(two, "two_list")
+        nc.sync.dma_start(d_word_table[:].bitcast(I32)[:, :FIRST], d_words_hbm[:, :FIRST])
+        for e in range(2):
+            nc.sync.dma_start(d_byte_table[:].bitcast(I32)[e:P:16, :], d_scales[0].bitcast(I32)[e:16:2, :])
+        nc.sync.dma_start(d_word_table[:].bitcast(I32)[:, FIRST:], d_words_hbm[:, FIRST:])
         for q in range(4):
             nc.sync.dma_start(
                 x_byte_table[:].bitcast(I32)[32 * q : 32 * q + 4, :],
@@ -76,12 +70,12 @@ def tile_picked_twkeysoftbpolar_none_p_kernel(
         for t in range(PACK):
             with nc.allow_non_contiguous_dma(reason="128 gains, one value a partition"):
                 nc.gpsimd.dma_start(gain[:, t, 0:1], gn_by_tile[t])
+        w1_raw = sbuf([P, PACK, S], F32, "w1_raw", tag="w_raw")
+        nc.sync.dma_start(w1_raw[:], w1.rearrange("(p j) c -> p j c", j=PACK))
         n2_list = load_list(n2, "n2_list")
         n1_list = load_list(n1, "n1_list")
         n3_list = load_list(n3, "n3_list")
         n4_list = load_list(n4, "n4_list")
-        w1_raw = sbuf([P, PACK, S], F32, "w1_raw", tag="w_raw")
-        nc.sync.dma_start(w1_raw[:], w1.rearrange("(p j) c -> p j c", j=PACK))
 
         d_gain = sbuf([P, PACK], F32, "d_gain")
         nc.gpsimd.tensor_scalar(d_gain[:], gain[:, :, 0], -0.0625, 0.0, ALU.mult, ALU.add)
@@ -93,13 +87,15 @@ def tile_picked_twkeysoftbpolar_none_p_kernel(
 
         d_bytes_picked = pick(d_byte_table, k1_list[:], U8, "d_bytes_picked")
         d_bytes = sbuf([P, S], U8, "d_bytes")
-        nc.vector.tensor_copy(
-            d_bytes[:].bitcast(I32).rearrange("p (t u) -> p t u", t=PACK),
-            d_bytes_picked[:].bitcast(I32).rearrange("p (u t) -> p t u", t=PACK),
-        )
-        nc.scalar.dma_start(
-            d_scale_plane[:].bitcast(I32)[0:SHIFTED, :], d_bytes[:].bitcast(I32)[SHIFT : SHIFT + SHIFTED, :]
-        )
+        for dealt in (d_scale_plane, d_bytes):
+            nc.vector.tensor_copy(
+                dealt[:].bitcast(I32).rearrange("p (t u) -> p t u", t=PACK),
+                d_bytes_picked[:].bitcast(I32).rearrange("p (u t) -> p t u", t=PACK),
+            )
+        for j in range(2):
+            nc.scalar.dma_start(
+                d_scale_plane[:].bitcast(I32)[2 + j : P : 32, :], d_bytes[:].bitcast(I32)[16 + j : P : 32, :]
+            )
         d_words_picked = pick(d_word_table, k1_list[:], U32, "d_words_picked")
         d_codes = sbuf([P, S], U32, "d_codes")
         nc.vector.tensor_copy(

from contextlib import ExitStack

import concourse.mybir as mybir

F32 = mybir.dt.float32
BF16 = mybir.dt.bfloat16
I32 = mybir.dt.int32
U32 = mybir.dt.uint32
U16 = mybir.dt.uint16
U8 = mybir.dt.uint8
FP8X4 = mybir.dt.float8_e4m3fn_x4
ACT = mybir.ActivationFunctionType
ALU = mybir.AluOpType

P = 128
PACK = 4
TABLE = 2048
S = 512
HALF = S // 2
FIRST = 256
PIECES = ((0, 256), (256, 128), (384, 128))
Y_ON_SCALAR = 3
FLOPS = 3 * 2 * 512 * 512 * 512


def tile_picked_twkeysoftbpolar_none_p_kernel(
    tc, x_words, x_scales, w1, d_words, d_scales, gn, w2, offs, k1, two, n1, n2, n3, n4, out
):
    nc = tc.nc
    with ExitStack() as ctx:
        lists = ctx.enter_context(tc.tile_pool(name="lists", bufs=1))
        keep = ctx.enter_context(tc.tile_pool(name="keep", bufs=1))
        psum = ctx.enter_context(tc.psum_pool(name="psum", bufs=1))

        def load_list(source, name):
            held = lists.tile(list(source.shape), U16, name=name)
            nc.sync.dma_start(held[:], source)
            return held

        def sbuf(shape, dtype, name, tag=""):
            return keep.tile(shape, dtype, name=name, tag=tag, align_bytes=64)

        d_byte_table = sbuf([P, TABLE], U8, "d_byte_table")
        x_byte_table = sbuf([P, TABLE], U8, "x_byte_table")
        d_word_table = sbuf([P, TABLE], U32, "d_word_table")
        x_word_table = sbuf([P, TABLE], U32, "x_word_table")
        d_scale_plane = sbuf([P, S], U8, "d_scale_plane")
        nc.vector.memset(d_byte_table[:].bitcast(I32), 0)
        nc.vector.memset(x_byte_table[:].bitcast(I32), 0)

        quarter = sbuf([P, 1], F32, "quarter")
        nc.gpsimd.memset(quarter[:], 0.25)

        d_words_hbm = d_words[0].rearrange("p n t -> p (n t)").bitcast(I32)
        k1_list = load_list(k1, "k1_list")
        two_list = load_list(two, "two_list")
        nc.sync.dma_start(d_word_table[:].bitcast(I32)[:, :FIRST], d_words_hbm[:, :FIRST])
        for e in range(2):
            nc.sync.dma_start(d_byte_table[:].bitcast(I32)[e:P:16, :], d_scales[0].bitcast(I32)[e:16:2, :])
        nc.sync.dma_start(d_word_table[:].bitcast(I32)[:, FIRST:], d_words_hbm[:, FIRST:])
        for q in range(4):
            nc.sync.dma_start(
                x_byte_table[:].bitcast(I32)[32 * q : 32 * q + 4, :],
                x_scales[0].bitcast(I32)[4 * q : 4 * q + 4, :],
            )
        nc.sync.dma_start(x_word_table[:].bitcast(I32), x_words[0].rearrange("p n t -> p (n t)").bitcast(I32))
        offs_list = load_list(offs, "offs_list")
        gain = sbuf([P, PACK, 8], F32, "gain")
        gn_by_tile = gn.rearrange("(u t r) o -> t u r o", t=PACK, r=4)
        for t in range(PACK):
            with nc.allow_non_contiguous_dma(reason="128 gains, one value a partition"):
                nc.gpsimd.dma_start(gain[:, t, 0:1], gn_by_tile[t])
        w1_raw = sbuf([P, PACK, S], F32, "w1_raw", tag="w_raw")
        nc.sync.dma_start(w1_raw[:], w1.rearrange("(p j) c -> p j c", j=PACK))
        n2_list = load_list(n2, "n2_list")
        n1_list = load_list(n1, "n1_list")
        n3_list = load_list(n3, "n3_list")
        n4_list = load_list(n4, "n4_list")

        d_gain = sbuf([P, PACK], F32, "d_gain")
        nc.gpsimd.tensor_scalar(d_gain[:], gain[:, :, 0], -0.0625, 0.0, ALU.mult, ALU.add)

        def pick(table, offsets, dtype, name):
            picked = sbuf([P, 16 * offsets.shape[1]], dtype, name)
            nc.vector.tensor_copy(picked[:], table[:].indirect(offsets))
            return picked

        d_bytes_picked = pick(d_byte_table, k1_list[:], U8, "d_bytes_picked")
        d_bytes = sbuf([P, S], U8, "d_bytes")
        for dealt in (d_scale_plane, d_bytes):
            nc.vector.tensor_copy(
                dealt[:].bitcast(I32).rearrange("p (t u) -> p t u", t=PACK),
                d_bytes_picked[:].bitcast(I32).rearrange("p (u t) -> p t u", t=PACK),
            )
        for j in range(2):
            nc.scalar.dma_start(
                d_scale_plane[:].bitcast(I32)[2 + j : P : 32, :], d_bytes[:].bitcast(I32)[16 + j : P : 32, :]
            )
        d_words_picked = pick(d_word_table, k1_list[:], U32, "d_words_picked")
        d_codes = sbuf([P, S], U32, "d_codes")
        nc.vector.tensor_copy(
            d_codes[:].rearrange("p (t u r) -> p t u r", t=PACK, r=4),
            d_words_picked[:].rearrange("p (u t r) -> p t u r", t=PACK, r=4),
        )

        def product(bank, width, lhs_codes, lhs_bytes, rhs_codes, rhs_bytes):
            acc = psum.tile([P, width], F32, name="acc", tag="bank%d" % bank)
            nc.tensor.matmul_mx(
                out=acc[:],
                lhsT=lhs_codes.bitcast(FP8X4),
                lhsT_scale=lhs_bytes,
                rhs=rhs_codes.bitcast(FP8X4),
                rhs_scale=rhs_bytes,
                start=True,
                stop=True,
            )
            return acc

        cols = [slice(P * t, P * (t + 1)) for t in range(PACK)]
        entries = [slice(half * HALF // 16, (half + 1) * HALF // 16) for half in range(2)]
        places = [slice(half * HALF, (half + 1) * HALF) for half in range(2)]
        tanh_d = sbuf([P, PACK, S], F32, "tanh_d")
        d_rows = [sbuf([P, S], F32, "d_rows%d" % t) for t in range(PACK)]
        for half in range(2):
            two_bytes = pick(x_byte_table, two_list[:, entries[half]], U8, "two_bytes%d" % half)
            two_codes = pick(x_word_table, two_list[:, entries[half]], U32, "two_codes%d" % half)
            for t in range(PACK):
                acc = product(
                    PACK * (1 - half) + t, HALF, d_codes[:, cols[t]], d_scale_plane[:, cols[t]], two_codes[:], two_bytes[:]
                )
                nc.scalar.activation(tanh_d[:, t, places[half]], acc[:], ACT.Tanh, scale=0.0625)
                nc.scalar.activation(d_rows[t][:, places[half]], acc[:], ACT.Copy, scale=d_gain[:, t : t + 1])

        x_bytes = pick(x_byte_table, offs_list[:], U8, "x_bytes")
        x_codes = pick(x_word_table, offs_list[:], U32, "x_codes")
        w1_bf = sbuf([P, PACK * S], BF16, "w1_bf", tag="w1_bf")
        nc.vector.tensor_copy(
            w1_bf[:].rearrange("p (t u r j) -> p t u j r", t=PACK, r=4, j=PACK),
            w1_raw[:].rearrange("p j (u t r) -> p t u j r", t=PACK, r=4),
        )
        w2_raw = sbuf([P, PACK, S], F32, "w2_raw", tag="w_raw")
        w2_by_slot = w2.rearrange("(u j r) c -> j u r c", j=PACK, r=4)
        for j in range(PACK):
            nc.sync.dma_start(w2_raw[:, j, :], w2_by_slot[j])

        def quantize(values, width, name):
            codes = sbuf([P, width], U32, name + "_codes")
            scale_bytes = sbuf([P, width], U8, name + "_bytes")
            nc.vector.quantize_mx(out=codes[:].bitcast(FP8X4), scales=scale_bytes[:], in_=values)
            return codes, scale_bytes

        y_acc = []
        for first in range(0, PACK, 2):
            w1_codes, w1_bytes = quantize(w1_bf[:, S * first : S * (first + 2)], 2 * P, "w1_%d" % first)
            for i in range(2):
                y_acc.append(
                    product(PACK + first + i, S, w1_codes[:, cols[i]], w1_bytes[:, cols[i]], x_codes[:], x_bytes[:])
                )

        y_rows = [sbuf([P, S], F32, "y_rows%d" % t, tag="y_rows%d" % t) for t in range(PACK)]
        for t in range(PACK):
            if t < Y_ON_SCALAR:
                nc.scalar.activation(y_rows[t][:], y_acc[t][:], ACT.Copy, scale=gain[:, t, 0:1])
            else:
                nc.vector.tensor_scalar_mul(y_rows[t][:], y_acc[t][:], gain[:, t, 0:1])

        y_got = [sbuf([P, PACK, width], F32, "y_got%d" % start) for start, width in PIECES]
        for got, (start, width) in zip(y_got, PIECES):
            piece_entries = slice(start // 16, (start + width) // 16)
            for t in range(PACK):
                nc.scalar.activation(got[:, t, :], y_rows[t][:].indirect(n1_list[:, piece_entries]), ACT.Copy)
        pull = sbuf([P, PACK, S], F32, "pull", tag="w1_bf")
        for half in range(2):
            for t in range(PACK):
                nc.vector.tensor_tensor(
                    pull[:, t, places[half]],
                    d_rows[t][:].indirect(n2_list[:, entries[half]]),
                    tanh_d[:, t, places[half]],
                    ALU.mult,
                )

        w2_by_tile = w2_raw[:].rearrange("p j (u t r) -> p t u j r", t=PACK, r=4)
        w2_mx = {}

        def w2_tile(t):
            w2_bf = sbuf([P, S], BF16, "w2_bf%d" % t, tag="y_rows%d" % t)
            nc.scalar.copy(w2_bf[:].rearrange("p (u r j) -> p u j r", r=4, j=PACK), w2_by_tile[:, t])
            w2_mx[t] = quantize(w2_bf[:], P, "w2_%d" % t)

        z_mx = []
        for got, (start, width) in zip(y_got, PIECES):
            z_bf = sbuf([P, PACK * width], BF16, "z_bf%d" % start)
            nc.vector.tensor_tensor(
                z_bf[:].rearrange("p (c i t) -> p c t i", i=4, t=PACK),
                got[:].rearrange("p t (c i) -> p c t i", i=4),
                pull[:, :, start : start + width].rearrange("p t (c i) -> p c t i", i=4),
                ALU.add,
            )
            z_mx.append(quantize(z_bf[:], width, "z_%d" % start))

        out_by_tile = out.rearrange("(u t r) c -> t u r c", t=PACK, r=4)

        def h_half(t, half):
            acc = psum.tile([P, HALF], F32, name="acc", tag="bank%d" % (2 * t + half))
            for (z_codes, z_bytes), (start, width) in zip(z_mx, PIECES):
                if start // HALF == half:
                    nc.tensor.matmul_mx(
                        out=acc[:, start % HALF : start % HALF + width],
                        lhsT=w2_mx[t][0][:].bitcast(FP8X4),
                        lhsT_scale=w2_mx[t][1][:],
                        rhs=z_codes[:].bitcast(FP8X4),
                        rhs_scale=z_bytes[:],
                        start=True,
                        stop=True,
                    )
            return acc

        def pair_up(first):
            pair = (first, first + 1)
            h_rows = {t: sbuf([P, S], F32, "h_rows%d" % t) for t in pair}
            result = {t: sbuf([P, S], F32, "result%d" % t) for t in pair}
            pb = {t: sbuf([P, HALF], F32, "pb%d" % t) for t in pair}
            minus_half_pa = {t: sbuf([P, HALF], F32, "minus_half_pa%d" % t) for t in pair}
            for t in pair:
                w2_tile(t)
                nc.scalar.copy(h_rows[t][:, places[0]], h_half(t, 0)[:])
            for t in pair:
                if t == 0:
                    nc.vector.tensor_copy(h_rows[t][:, places[1]], h_half(t, 1)[:])
                    nc.vector.tensor_copy(pb[t][:], h_rows[t][:].indirect(n4_list[:]))
                else:
                    nc.scalar.copy(h_rows[t][:, places[1]], h_half(t, 1)[:])
            for t in pair:
                nc.scalar.activation(minus_half_pa[t][:], h_rows[t][:].indirect(n3_list[:]), ACT.Copy, scale=-0.5)
                if t > 0:
                    nc.scalar.activation(pb[t][:], h_rows[t][:].indirect(n4_list[:]), ACT.Copy)
                rb = sbuf([P, HALF], F32, "rb%d" % t)
                adder = nc.vector if t == 0 else nc.gpsimd
                adder.tensor_tensor(rb[:], pb[t][:], minus_half_pa[t][:], ALU.add)
                nc.vector.tensor_copy(result[t][:].indirect(n4_list[:]), rb[:])
            radius_sq = {t: sbuf([P, HALF], F32, "radius_sq%d" % t) for t in pair}
            for t in pair:
                pa_sq = sbuf([P, HALF], F32, "pa_sq%d" % t)
                pb_sq = sbuf([P, HALF], F32, "pb_sq%d" % t)
                nc.scalar.activation(pa_sq[:], minus_half_pa[t][:], ACT.Square, scale=-2.0)
                nc.scalar.activation(pb_sq[:], pb[t][:], ACT.Square)
                nc.gpsimd.tensor_tensor(radius_sq[t][:], pa_sq[:], pb_sq[:], ALU.add)
            for t in pair:
                ra = sbuf([P, HALF], F32, "ra%d" % t)
                nc.scalar.activation(ra[:], radius_sq[t][:], ACT.Sqrt, bias=quarter[:])
                nc.vector.tensor_copy(result[t][:].indirect(n3_list[:]), ra[:])
                nc.sync.dma_start(out_by_tile[t], result[t][:])

        for first in range(0, PACK, 2):
            pair_up(first)
